import numpy as np
CORES = [7,15,23,31,39,47,55,63,135,143,151,159,167,175,183,191]
N = 16
def setup_inputs(rng):
    return {"x": rng.standard_normal((N, 128, 256), dtype=np.float32)}
def reference(x):
    s = (x.sum(axis=0, dtype=np.float64) / N).astype(x.dtype)
    b = 256 // N
    return {"y": np.stack([s[:, r * b:(r + 1) * b] for r in range(N)])}

@@ -1,0 +1,71 @@
+from concourse.bass import RemoteDMATransfer, DstId
+from concourse.mybir import AluOpType
+
+SCRATCH = {
+    "xs": ("sbuf", [128, 256], "float32"),
+    "l1": ("sbuf", [128, 256], "float32"),
+    "p1": ("sbuf", [128, 128], "float32"),
+    "p2": ("sbuf", [128, 64], "float32"),
+    "l2": ("sbuf", [128, 64], "float32"),
+    "q1": ("sbuf", [128, 32], "float32"),
+    "q2": ("sbuf", [128, 16], "float32"),
+    "sc": ("sbuf", [128, 16], "float32"),
+    "res": ("sbuf", [128, 16], "float32"),
+}
+SEMAPHORES = ["loaded", "stored", "sent", "arr1", "arr2", "vc", "v0", "v1", "v2", "v3", "v4", "v5", "v6"]
+
+MASKS = (0x30, 0xC0, 0x0F)
+ARRIVE = 2 + 2 + 4
+
+
+def rank_program(g, core, T, topo):
+    r = T.rank_of(core)
+    if r is None:
+        return
+    S = T.sem
+    v = g.vector
+    a, b = divmod(r, 4)
+    add = AluOpType.add
+
+    def send(pieces, sem):
+        trs = []
+        for k, (dst_rank, src, dst) in enumerate(pieces):
+            rid, pid = topo.addr(T.cores[dst_rank], core)
+            trs.append(RemoteDMATransfer(dst_ids=[DstId(rid=rid, pnc=pid)], dma_engine_mask=MASKS[k], remote_sem=sem,
+                                         src=src, dst=dst))
+        g.remote_dma_fused(trs, local_sem=S.sent)
+
+    g.sync.dma_start(T.xs[:], T.x[:]).then_inc(S.loaded, 16)
+    v.memset(T.sc[:], 1.0 / 16).then_inc(S.vc, 1)
+
+    g.wait_ge(S.loaded, 16)
+    send([(4 * ((a + d) % 4) + b, T.xs[:, 64 * ((a + d) % 4):64 * ((a + d) % 4) + 64], T.l1[:, 64 * (d - 1):64 * d])
+          for d in (1, 2, 3)], S.arr1)
+
+    v.wait_ge(S.loaded, 16)
+    v.tensor_copy(T.l1[:, 192:256], T.xs[:, 64 * a:64 * a + 64]).then_inc(S.v0, 1)
+    v.wait_ge(S.v0, 1)
+    v.wait_ge(S.arr1, ARRIVE)
+    v.tensor_tensor(T.p1[:], T.l1[:, 0:128], T.l1[:, 128:256], add).then_inc(S.v1, 1)
+    v.wait_ge(S.v1, 1)
+    v.tensor_tensor(T.p2[:], T.p1[:, 0:64], T.p1[:, 64:128], add).then_inc(S.v2, 1)
+
+    g.wait_ge(S.v2, 1)
+    send([(4 * a + (b ^ e), T.p2[:, 16 * (b ^ e):16 * (b ^ e) + 16], T.l2[:, 16 * (e - 1):16 * e])
+          for e in (1, 2, 3)], S.arr2)
+
+    v.wait_ge(S.v2, 1)
+    v.tensor_copy(T.l2[:, 48:64], T.p2[:, 16 * b:16 * b + 16]).then_inc(S.v3, 1)
+    v.wait_ge(S.v3, 1)
+    v.wait_ge(S.arr2, ARRIVE)
+    v.tensor_tensor(T.q1[:], T.l2[:, 0:32], T.l2[:, 32:64], add).then_inc(S.v4, 1)
+    v.wait_ge(S.v4, 1)
+    v.tensor_tensor(T.q2[:], T.q1[:, 0:16], T.q1[:, 16:32], add).then_inc(S.v5, 1)
+    v.wait_ge(S.v5, 1)
+    v.wait_ge(S.vc, 1)
+    v.tensor_tensor(T.res[:], T.q2[:], T.sc[:], AluOpType.mult).then_inc(S.v6, 1)
+
+    g.sync.wait_ge(S.v6, 1)
+    g.sync.dma_start(T.y[:], T.res[:]).then_inc(S.stored, 16)
+    g.sync.wait_ge(S.stored, 16)
+    g.wait_ge(S.sent, 2 * ARRIVE)

@@ -3,69 +3,88 @@ from concourse.mybir import AluOpType
 
 SCRATCH = {
     "xs": ("sbuf", [128, 256], "float32"),
-    "l1": ("sbuf", [128, 256], "float32"),
-    "p1": ("sbuf", [128, 128], "float32"),
-    "p2": ("sbuf", [128, 64], "float32"),
-    "l2": ("sbuf", [128, 64], "float32"),
-    "q1": ("sbuf", [128, 32], "float32"),
-    "q2": ("sbuf", [128, 16], "float32"),
+    "hl": ("sbuf", [128, 64], "float32"),
+    "ld": ("sbuf", [128, 256], "float32"),
+    "e1": ("sbuf", [128, 32], "float32"),
+    "u1": ("sbuf", [128, 96], "float32"),
+    "u2": ("sbuf", [128, 64], "float32"),
+    "u3": ("sbuf", [128, 32], "float32"),
+    "u4": ("sbuf", [128, 16], "float32"),
     "sc": ("sbuf", [128, 16], "float32"),
     "res": ("sbuf", [128, 16], "float32"),
 }
-SEMAPHORES = ["loaded", "stored", "sent", "arr1", "arr2", "vc", "v0", "v1", "v2", "v3", "v4", "v5", "v6"]
+SEMAPHORES = ["loaded", "stored", "sent", "hand", "early", "late", "vc", "v0", "v1", "v2", "v3", "v4", "v5", "v6", "v7"]
 
-MASKS = (0x30, 0xC0, 0x0F)
-ARRIVE = 2 + 2 + 4
+HELPER = {1: 2, 2: 3, 3: 6}
+
+
+def fused(g, core, T, topo, pieces, sem):
+    trs = []
+    for dst_core, mask, src, dst in pieces:
+        rid, pid = topo.addr(dst_core, core)
+        trs.append(RemoteDMATransfer(dst_ids=[DstId(rid=rid, pnc=pid)], dma_engine_mask=mask, remote_sem=sem,
+                                     src=src, dst=dst))
+    g.remote_dma_fused(trs, local_sem=T.sem.sent)
+
+
+def helper_program(g, core, T, topo, r, d):
+    S = T.sem
+    a, b = divmod(r, 4)
+    a2 = (a + d) % 4
+    col = 64 * (d - 1) + 16 * b
+    g.wait_ge(S.hand, 4)
+    fused(g, core, T, topo,
+          [(T.cores[4 * a2 + j], 0x03 << (2 * j), T.hl[:, 16 * j:16 * j + 16], T.ld[:, col:col + 16]) for j in range(4)],
+          S.late)
+    g.wait_ge(S.sent, 8)
 
 
 def rank_program(g, core, T, topo):
     r = T.rank_of(core)
     if r is None:
+        owner = T.rank_of(core - core % 8 + 7)
+        for d, h in HELPER.items():
+            if owner is not None and core % 8 == h:
+                helper_program(g, core, T, topo, owner, d)
         return
     S = T.sem
     v = g.vector
     a, b = divmod(r, 4)
     add = AluOpType.add
 
-    def send(pieces, sem):
-        trs = []
-        for k, (dst_rank, src, dst) in enumerate(pieces):
-            rid, pid = topo.addr(T.cores[dst_rank], core)
-            trs.append(RemoteDMATransfer(dst_ids=[DstId(rid=rid, pnc=pid)], dma_engine_mask=MASKS[k], remote_sem=sem,
-                                         src=src, dst=dst))
-        g.remote_dma_fused(trs, local_sem=S.sent)
-
     g.sync.dma_start(T.xs[:], T.x[:]).then_inc(S.loaded, 16)
     v.memset(T.sc[:], 1.0 / 16).then_inc(S.vc, 1)
 
     g.wait_ge(S.loaded, 16)
-    send([(4 * ((a + d) % 4) + b, T.xs[:, 64 * ((a + d) % 4):64 * ((a + d) % 4) + 64], T.l1[:, 64 * (d - 1):64 * d])
-          for d in (1, 2, 3)], S.arr1)
+    fused(g, core, T, topo,
+          [(core - 7 + HELPER[d], 0x00F0 << (4 * (d - 1)), T.xs[:, 64 * ((a + d) % 4):64 * ((a + d) % 4) + 64], T.hl[:])
+           for d in (1, 2, 3)], S.hand)
+    own = 192 + 16 * b
+    fused(g, core, T, topo,
+          [(T.cores[4 * a + (b ^ e)], m, T.xs[:, 16 * (4 * a + (b ^ e)):16 * (4 * a + (b ^ e)) + 16], T.ld[:, own:own + 16])
+           for e, m in ((3, 0x03), (1, 0x04), (2, 0x08))], S.early)
 
     v.wait_ge(S.loaded, 16)
-    v.tensor_copy(T.l1[:, 192:256], T.xs[:, 64 * a:64 * a + 64]).then_inc(S.v0, 1)
+    v.tensor_copy(T.ld[:, own:own + 16], T.xs[:, 16 * r:16 * r + 16]).then_inc(S.v0, 1)
     v.wait_ge(S.v0, 1)
-    v.wait_ge(S.arr1, ARRIVE)
-    v.tensor_tensor(T.p1[:], T.l1[:, 0:128], T.l1[:, 128:256], add).then_inc(S.v1, 1)
+    v.wait_ge(S.early, 4)
+    v.tensor_tensor(T.e1[:], T.ld[:, 192:224], T.ld[:, 224:256], add).then_inc(S.v1, 1)
     v.wait_ge(S.v1, 1)
-    v.tensor_tensor(T.p2[:], T.p1[:, 0:64], T.p1[:, 64:128], add).then_inc(S.v2, 1)
-
-    g.wait_ge(S.v2, 1)
-    send([(4 * a + (b ^ e), T.p2[:, 16 * (b ^ e):16 * (b ^ e) + 16], T.l2[:, 16 * (e - 1):16 * e])
-          for e in (1, 2, 3)], S.arr2)
-
-    v.wait_ge(S.v2, 1)
-    v.tensor_copy(T.l2[:, 48:64], T.p2[:, 16 * b:16 * b + 16]).then_inc(S.v3, 1)
+    v.tensor_tensor(T.u2[:, 48:64], T.e1[:, 0:16], T.e1[:, 16:32], add).then_inc(S.v2, 1)
+    v.wait_ge(S.late, 24)
+    v.tensor_tensor(T.u1[:], T.ld[:, 0:96], T.ld[:, 96:192], add).then_inc(S.v3, 1)
     v.wait_ge(S.v3, 1)
-    v.wait_ge(S.arr2, ARRIVE)
-    v.tensor_tensor(T.q1[:], T.l2[:, 0:32], T.l2[:, 32:64], add).then_inc(S.v4, 1)
+    v.tensor_tensor(T.u2[:, 0:48], T.u1[:, 0:48], T.u1[:, 48:96], add).then_inc(S.v4, 1)
     v.wait_ge(S.v4, 1)
-    v.tensor_tensor(T.q2[:], T.q1[:, 0:16], T.q1[:, 16:32], add).then_inc(S.v5, 1)
+    v.wait_ge(S.v2, 1)
+    v.tensor_tensor(T.u3[:], T.u2[:, 0:32], T.u2[:, 32:64], add).then_inc(S.v5, 1)
     v.wait_ge(S.v5, 1)
+    v.tensor_tensor(T.u4[:], T.u3[:, 0:16], T.u3[:, 16:32], add).then_inc(S.v6, 1)
+    v.wait_ge(S.v6, 1)
     v.wait_ge(S.vc, 1)
-    v.tensor_tensor(T.res[:], T.q2[:], T.sc[:], AluOpType.mult).then_inc(S.v6, 1)
+    v.tensor_tensor(T.res[:], T.u4[:], T.sc[:], AluOpType.mult).then_inc(S.v7, 1)
 
-    g.sync.wait_ge(S.v6, 1)
+    g.sync.wait_ge(S.v7, 1)
     g.sync.dma_start(T.y[:], T.res[:]).then_inc(S.stored, 16)
     g.sync.wait_ge(S.stored, 16)
-    g.wait_ge(S.sent, 2 * ARRIVE)
+    g.wait_ge(S.sent, 12 + 4)

from concourse.bass import RemoteDMATransfer, DstId
from concourse.mybir import AluOpType

SCRATCH = {
    "xs": ("sbuf", [128, 256], "float32"),
    "hl": ("sbuf", [128, 64], "float32"),
    "ld": ("sbuf", [128, 256], "float32"),
    "e1": ("sbuf", [128, 32], "float32"),
    "u1": ("sbuf", [128, 96], "float32"),
    "u2": ("sbuf", [128, 64], "float32"),
    "u3": ("sbuf", [128, 32], "float32"),
    "u4": ("sbuf", [128, 16], "float32"),
    "sc": ("sbuf", [128, 16], "float32"),
    "res": ("sbuf", [128, 16], "float32"),
}
SEMAPHORES = ["loaded", "stored", "sent", "hand", "early", "late", "vc", "v0", "v1", "v2", "v3", "v4", "v5", "v6", "v7"]

HELPER = {1: 2, 2: 3, 3: 6}


def fused(g, core, T, topo, pieces, sem):
    trs = []
    for dst_core, mask, src, dst in pieces:
        rid, pid = topo.addr(dst_core, core)
        trs.append(RemoteDMATransfer(dst_ids=[DstId(rid=rid, pnc=pid)], dma_engine_mask=mask, remote_sem=sem,
                                     src=src, dst=dst))
    g.remote_dma_fused(trs, local_sem=T.sem.sent)


def helper_program(g, core, T, topo, r, d):
    S = T.sem
    a, b = divmod(r, 4)
    a2 = (a + d) % 4
    col = 64 * (d - 1) + 16 * b
    g.wait_ge(S.hand, 4)
    fused(g, core, T, topo,
          [(T.cores[4 * a2 + j], 0x03 << (2 * j), T.hl[:, 16 * j:16 * j + 16], T.ld[:, col:col + 16]) for j in range(4)],
          S.late)
    g.wait_ge(S.sent, 8)


def rank_program(g, core, T, topo):
    r = T.rank_of(core)
    if r is None:
        owner = T.rank_of(core - core % 8 + 7)
        for d, h in HELPER.items():
            if owner is not None and core % 8 == h:
                helper_program(g, core, T, topo, owner, d)
        return
    S = T.sem
    v = g.vector
    a, b = divmod(r, 4)
    add = AluOpType.add

    g.sync.dma_start(T.xs[:], T.x[:]).then_inc(S.loaded, 16)
    v.memset(T.sc[:], 1.0 / 16).then_inc(S.vc, 1)

    g.wait_ge(S.loaded, 16)
    fused(g, core, T, topo,
          [(core - 7 + HELPER[d], 0x00F0 << (4 * (d - 1)), T.xs[:, 64 * ((a + d) % 4):64 * ((a + d) % 4) + 64], T.hl[:])
           for d in (1, 2, 3)], S.hand)
    own = 192 + 16 * b
    fused(g, core, T, topo,
          [(T.cores[4 * a + (b ^ e)], m, T.xs[:, 16 * (4 * a + (b ^ e)):16 * (4 * a + (b ^ e)) + 16], T.ld[:, own:own + 16])
           for e, m in ((3, 0x03), (1, 0x04), (2, 0x08))], S.early)

    v.wait_ge(S.loaded, 16)
    v.tensor_copy(T.ld[:, own:own + 16], T.xs[:, 16 * r:16 * r + 16]).then_inc(S.v0, 1)
    v.wait_ge(S.v0, 1)
    v.wait_ge(S.early, 4)
    v.tensor_tensor(T.e1[:], T.ld[:, 192:224], T.ld[:, 224:256], add).then_inc(S.v1, 1)
    v.wait_ge(S.v1, 1)
    v.tensor_tensor(T.u2[:, 48:64], T.e1[:, 0:16], T.e1[:, 16:32], add).then_inc(S.v2, 1)
    v.wait_ge(S.late, 24)
    v.tensor_tensor(T.u1[:], T.ld[:, 0:96], T.ld[:, 96:192], add).then_inc(S.v3, 1)
    v.wait_ge(S.v3, 1)
    v.tensor_tensor(T.u2[:, 0:48], T.u1[:, 0:48], T.u1[:, 48:96], add).then_inc(S.v4, 1)
    v.wait_ge(S.v4, 1)
    v.wait_ge(S.v2, 1)
    v.tensor_tensor(T.u3[:], T.u2[:, 0:32], T.u2[:, 32:64], add).then_inc(S.v5, 1)
    v.wait_ge(S.v5, 1)
    v.tensor_tensor(T.u4[:], T.u3[:, 0:16], T.u3[:, 16:32], add).then_inc(S.v6, 1)
    v.wait_ge(S.v6, 1)
    v.wait_ge(S.vc, 1)
    v.tensor_tensor(T.res[:], T.u4[:], T.sc[:], AluOpType.mult).then_inc(S.v7, 1)

    g.sync.wait_ge(S.v7, 1)
    g.sync.dma_start(T.y[:], T.res[:]).then_inc(S.stored, 16)
    g.sync.wait_ge(S.stored, 16)
    g.wait_ge(S.sent, 12 + 4)
